import numpy as np
import ml_dtypes


def mxq(x, axis, fmt="e4m3"):
    dtype, down = {"e4m3": (ml_dtypes.float8_e4m3fn, 7), "e5m2": (ml_dtypes.float8_e5m2, 14)}[fmt]
    v = np.moveaxis(np.asarray(x, np.float32).astype(ml_dtypes.bfloat16).astype(np.float64), axis, -1)
    blocks = v.reshape(v.shape[:-1] + (-1, 32))
    amax = np.abs(blocks).max(-1, keepdims=True)
    byte = np.maximum(np.where(amax > 0, np.frexp(amax)[1] - 1 + 127, 0) - down, 1)
    scale = np.exp2(byte - 127.0)
    codes = (blocks / scale).astype(np.float32).astype(dtype).astype(np.float64)
    return np.moveaxis((codes * scale).reshape(v.shape), -1, axis)


WIDE = False


def mx_kscale(k):
    if not WIDE:
        return np.ones(k)
    levels = np.array([10, -10, 5, -5, 0])
    if k % 512:
        return np.exp2(np.random.permutation(np.resize(levels, k // 32))).repeat(32)
    a = np.empty((k // 512, 16))
    for p in range(k // 512):
        a[p, :8] = np.random.permutation(np.resize(levels, 8))
        for g in range(8):
            far = levels[np.abs(levels - a[p, g]) >= 10]
            a[p, g + 8] = far[np.random.randint(len(far))]
    return np.exp2(a.ravel()).repeat(32)


BF16 = ml_dtypes.bfloat16


def bf(x):
    return np.asarray(x, np.float32).astype(BF16)


def f64(x):
    return np.asarray(x).astype(np.float64)


E2M1 = np.array([0.0, 0.5, 1.0, 1.5, 2.0, 3.0, 4.0, 6.0, -0.0, -0.5, -1.0, -1.5, -2.0, -3.0, -4.0, -6.0])


def pack_weight(w, fmt):
    k, n = w.shape
    w = f64(bf(w)).reshape(k // 32, 32, n)
    amax = np.abs(w).max(1)
    if fmt == "e4m3":
        byte = np.frexp(amax)[1] - 1 + 127 - 7
    else:
        mant, ex = np.frexp(amax / 6.0)
        byte = np.where(mant > 0.5, ex, ex - 1) + 127
    byte = np.clip(np.where(amax > 0, byte, 1), 1, 254)
    scaled = (w * np.exp2(127.0 - byte)[:, None, :]).reshape(k, n).astype(np.float32)
    by_word = np.ascontiguousarray(scaled.reshape(k // 512, 128, 4, n).transpose(0, 1, 3, 2))
    if fmt == "e4m3":
        words = by_word.astype(ml_dtypes.float8_e4m3fn).view(np.uint8)
    else:
        c = by_word.astype(ml_dtypes.float4_e2m1fn).view(np.uint8) & 0xF
        words = c[..., 0::2] | (c[..., 1::2] << 4)
    return np.ascontiguousarray(words), np.ascontiguousarray(byte.astype(np.uint8).reshape(k // 512, 16, n))


def unpack_weight(words, scales, fmt):
    g, p, n, _ = words.shape
    if fmt == "e4m3":
        vals = np.ascontiguousarray(words).view(ml_dtypes.float8_e4m3fn).astype(np.float64)
    else:
        nib = np.empty((g, p, n, 4), np.uint8)
        nib[..., 0::2] = words & 0xF
        nib[..., 1::2] = words >> 4
        vals = E2M1[nib]
    vals = vals * np.repeat(np.exp2(scales.astype(np.float64) - 127.0), 8, axis=1)[..., None]
    return vals.transpose(0, 1, 3, 2).reshape(g * 512, n)
def pack4(w):
    words, scales = pack_weight(w, "e2m1")
    return words.reshape(words.shape[0], 128, -1), scales


def unpack4(words, scales):
    return unpack_weight(words.reshape(words.shape[0], 128, -1, 2), scales, "e2m1")


def planes(Y):
    n, m = Y.shape
    b = f64(bf(Y)).reshape(n // 32, 32, m)
    amax = np.abs(b).max(1)
    byte = np.clip(np.where(amax > 0, np.frexp(amax)[1] - 1 + 127 - 7, 1), 1, 254)
    codes = (b * np.exp2(127.0 - byte)[:, None, :]).reshape(n, m).astype(np.float32).astype(ml_dtypes.float8_e4m3fn).view(np.uint8)
    words = codes.reshape(n // 512, 128, 4, m).transpose(0, 1, 3, 2)
    return np.ascontiguousarray(words), np.ascontiguousarray(byte.astype(np.uint8).reshape(n // 512, 16, m))


M, N, F = 1024, 2048, 1024

def setup_inputs():
    s = mx_kscale(N)
    t = mx_kscale(F)
    spread = np.exp(0.7 * np.random.randn(N))
    states = np.random.randn(M, N) * s
    gain = np.random.randn(N, F) / np.sqrt(N) / s[:, None] * t
    u_max = (0.8 + 0.6 * np.random.rand(F)) * t
    u_min = -(0.6 + 0.6 * np.random.rand(F)) * t
    inmat = 1.3 * np.random.randn(F, N) / np.sqrt(F) * spread / t[:, None]
    slope = -(0.3 + 0.4 * np.random.rand(N)) * spread / s
    offset = 0.3 * np.random.randn(N) * spread
    gain_words, gain_scales = pack4(gain)
    inmat_words, inmat_scales = pack4(inmat)
    return {"states": bf(states), "gain_words": gain_words, "gain_scales": gain_scales,
            "u_min": bf(u_min), "u_max": bf(u_max),
            "inmat_words": inmat_words, "inmat_scales": inmat_scales,
            "slope": bf(slope), "offset": bf(offset)}

def reference(states, gain_words, gain_scales, u_min, u_max, inmat_words, inmat_scales, slope, offset):
    x = f64(states)
    v = mxq(x, 1, "e4m3") @ unpack4(gain_words, gain_scales)
    u = np.minimum(np.maximum(v, f64(u_min)), f64(u_max))
    forced = mxq(u, 1, "e4m3") @ unpack4(inmat_words, inmat_scales)
    y = forced + x * f64(slope) + f64(offset)
    Y = y.T
    words, scales = planes(Y)
    return y, words, scales

from contextlib import ExitStack

import concourse.mybir as mybir
from concourse.masks import make_identity

M, N, F = 1024, 2048, 1024
FLOPS = 2 * M * N * F * 2

F32 = mybir.dt.float32
BF16 = mybir.dt.bfloat16
I32 = mybir.dt.int32
U32 = mybir.dt.uint32
U8 = mybir.dt.uint8
FP8X4 = mybir.dt.float8_e4m3fn_x4
FP4X4 = mybir.dt.float4_e2m1fn_x4
ALU = mybir.AluOpType
ACT = mybir.ActivationFunctionType
P = 128

ORDER = """
XT:0,0 XT:0,1 CX:0,0 CX:0,1 QX:0,0 QX:0,1 S1:0,0 XT:1,0 XT:1,1 CU:0,0 CX:1,0 CX:1,1 QX:1,0 QX:1,1
S1:0,1 CU:0,1 XT:2,0 XT:2,1 CX:2,0 CX:2,1 QX:2,0 QX:2,1 S1:1,0 S1:1,1 CU:1,0 CU:1,1 UT:0 XT:3,0
XT:3,1 MX:0 PW:0 CX:3,0 CX:3,1 MN:0 QX:3,0 QX:3,1 QU:0 PW:1 S1:2,0 S1:2,1 DR:1,0,0 CU:2,0
DR:1,1,0 CU:2,1 DR:1,2,0 UT:1 XT:4,0 XT:4,1 MX:1 DR:0,0,1 DR:0,1,1 CX:4,0 CX:4,1 MN:1 QX:4,0 QX:4,1
QU:1 DR:0,2,1 DR:0,3,1 S1:3,0 S1:3,1 DR:1,3,0 CU:3,0 DR:2,0,0 CU:3,1 DR:2,1,0 UT:2 XT:5,0 XT:5,1 MX:2
PS:0 CX:5,0 CX:5,1 MN:2 QX:5,0 QX:5,1 QU:2 PS:1 S1:4,0 S1:4,1 DR:2,2,0 CU:4,0 DR:2,3,0 CU:4,1
DR:3,0,0 UT:3 XT:6,0 XT:6,1 MX:3 PW:2 CX:6,0 CX:6,1 MN:3 QX:6,0 QX:6,1 QU:3 PS:2 S1:5,0
S1:5,1 DR:3,1,0 CU:5,0 DR:3,2,0 CU:5,1 DR:3,3,0 UT:4 XT:7,0 XT:7,1 MX:4 PW:3 CX:7,0 CX:7,1 MN:4
QX:7,0 QX:7,1 QU:4 PS:3 S1:6,0 S1:6,1 DR:4,0,0 CU:6,0 DR:4,1,0 CU:6,1 DR:4,2,0 DR:4,3,0 S2:0,0 AD:0,0
S2:0,1 AD:0,1 S2:0,2 AD:0,2 S2:0,3 AD:0,3 UT:5 UT:6 MX:5 MX:6 MN:5 MN:6 QU:5 QU:6
S1:7,0 S1:7,1 DR:5,0,0 DR:5,1,0 CU:7,0 DR:5,2,0 DR:5,3,0 CU:7,1 DR:6,0,0 DR:6,1,0 S2:1,0 AD:1,0 S2:1,1 AD:1,1
S2:1,2 AD:1,2 S2:1,3 AD:1,3 UT:7 YT:0,0 YT:0,1 YT:0,2 YT:0,3 MX:7 IL:0,1 IL:0,0 CY:0,0,0 SY:0,0,1
CY:0,1,0 SY:0,1,2 CY:0,2,0 SY:0,2,3 CY:0,3,0 SY:0,3,4 MN:7 QY:0 SC:0,0,4 QU:7 DR:6,2,0 DR:6,3,0 S2:2,0 AD:2,0
S2:2,1 AD:2,1 S2:2,2 AD:2,2 S2:2,3 AD:2,3 YT:1,0 YT:1,1 YT:1,2 YT:1,3 IL:1,1 IL:1,0 CY:1,0,0 SY:1,0,1
CY:1,1,0 SY:1,1,2 CY:1,2,0 SY:1,2,3 CY:1,3,0 SY:1,3,4 DR:7,0,0 S2:3,0 AD:3,0 QY:1 SC:1,0,4 S2:3,1 AD:3,1 S2:3,2
AD:3,2 S2:3,3 AD:3,3 YT:2,0 YT:2,1 YT:2,2 YT:2,3 IL:2,1 IL:2,0 CY:2,0,0 SY:2,0,1 CY:2,1,0 SY:2,1,2 CY:2,2,0
SY:2,2,3 CY:2,3,0 SY:2,3,4 DR:7,1,0 S2:4,0 AD:4,0 QY:2 SC:2,0,4 S2:4,1 AD:4,1 S2:4,2 AD:4,2 S2:4,3 AD:4,3
YT:3,0 YT:3,1 YT:3,2 YT:3,3 IL:3,1 IL:3,0 CY:3,0,0 SY:3,0,1 CY:3,1,0 SY:3,1,2 CY:3,2,0 SY:3,2,3 CY:3,3,0 SY:3,3,4
DR:7,2,0 S2:5,0 AD:5,0 QY:3 SC:3,0,4 SS:0,0,4 S2:5,1 AD:5,1 S2:5,2 AD:5,2 S2:5,3 AD:5,3 YT:4,0 YT:4,1
YT:4,2 YT:4,3 IL:4,1 IL:4,0 CY:4,0,0 SY:4,0,1 CY:4,1,0 SY:4,1,2 CY:4,2,0 SY:4,2,3 CY:4,3,0 SY:4,3,4 DR:7,3,0 S2:6,0
AD:6,0 QY:4 SC:4,0,4 S2:6,1 AD:6,1 S2:6,2 AD:6,2 S2:6,3 AD:6,3 YT:5,0 YT:5,1 YT:5,2 YT:5,3 IL:5,1
IL:5,0 CY:5,0,0 SY:5,0,1 CY:5,1,0 SY:5,1,2 CY:5,2,0 SY:5,2,3 CY:5,3,0 SY:5,3,4 Z2:7,0 ZA:7,0 QY:5 SC:5,0,4 YT:6,0
YT:6,1 YT:6,2 YT:6,3 IL:6,1 IL:6,0 CY:6,0,0 SY:6,0,1 CY:6,1,0 SY:6,1,2 Z2:7,1 ZA:7,1 ZT:7,0 Z2:7,2 CY:6,2,0
SY:6,2,3 QY:6 SC:6,0,4 SS:1,0,3 ZA:7,2 CY:6,3,0 SY:6,3,4 ZI:7,0 ZT:7,1 Z2:7,3 ZA:7,3 ZI:7,1 ZQ:7,0 ZI:7,2
CY:7,0,0 SY:7,0,1 CY:7,1,0 SY:7,1,2 ZQ:7,1 SC:7,0,2 ZT:7,2 ZT:7,3 ZI:7,3 ZQ:7,2 CY:7,2,0 SY:7,2,3 CY:7,3,0 SY:7,3,4
ZQ:7,3 SC:7,2,4 SS:1,3,4
""".split()
SPLIT = [352, 352, 352, 352, 352, 352, 352, 352]


def tile_saturated_feedback_velocity_h1_kernel(
    tc, states, gain_words, gain_scales, u_min, u_max, inmat_words, inmat_scales, slope, offset, out_0, out_1, out_2
):
    nc = tc.nc
    with ExitStack() as ctx:
        keep = ctx.enter_context(tc.tile_pool(name="keep", bufs=1))
        ring = ctx.enter_context(tc.tile_pool(name="ring", bufs=3))
        ypool = ctx.enter_context(tc.tile_pool(name="ypool", bufs=7))
        xpool = ctx.enter_context(tc.tile_pool(name="xpool", bufs=6))
        psum = ctx.enter_context(tc.psum_pool(name="psum", bufs=1))
        ctx.enter_context(tc.manual_schedule())

        ident = keep.tile([P, P], F32)
        slope_bf = keep.tile([P, 4, 4], BF16)
        slope_f = keep.tile([P, 4, 4], F32)
        offset_bf = keep.tile([P, 4, 4], BF16)
        lo = keep.tile([P, 2, 4], BF16)
        hi = keep.tile([P, 2, 4], BF16)
        x_rows = [xpool.tile([P, N], BF16, name="x_rows", align_bytes=64) for i in range(8)]
        g_words = [keep.tile([P, 4, 1024], U8, name="g_words%d" % c, align_bytes=64) for c in range(2)]
        g_scales = keep.tile([P, 4, F], U8, align_bytes=64)
        b_raw = [keep.tile([P, 2, 2048], U8, name="b_raw%d" % k, align_bytes=64) for k in range(2)]
        bs_raw = keep.tile([P, 2, N], U8, align_bytes=64)
        b_words = keep.tile([P, 4, 2, 1024], U8, align_bytes=64)
        b_scales = keep.tile([P, 4, 2, 512], U8, align_bytes=64)
        x_t = [keep.tile([P, 4, 4, P, 4], BF16, name="x_t%d" % h, align_bytes=64) for h in range(2)]
        u_codes = [keep.tile([P, 2, 512], U32, name="u_codes%d" % h, align_bytes=64) for h in range(2)]
        u_scales = [keep.tile([P, 2, 512], U8, name="u_scales%d" % h, align_bytes=64) for h in range(2)]
        y_scales = [keep.tile([P, 4, 512], U8, name="y_scales%d" % h, align_bytes=64) for h in range(2)]

        live = {}
        count = [0]

        def new_bank(key):
            b = count.pop()
            count.append(b + 1)
            live[key] = psum.tile([P, 512], F32, name="bank%d" % (b % 8), tag="bank%d" % (b % 8))
            return live[key]

        def load_scales(plane, scales):
            for q in range(4):
                nc.sync.dma_start(
                    out=plane[32 * q : 32 * q + 4].bitcast(I32),
                    in_=scales[:, 4 * q : 4 * q + 4, :].bitcast(I32).rearrange("g r w -> r g w"),
                )

        def load_x(i, lo_col, hi_col):
            nc.sync.dma_start(out=x_rows[i][:, lo_col:hi_col], in_=states[P * i : P * (i + 1), lo_col:hi_col])

        def load_vec(dst, vec):
            nc.sync.dma_start(out=dst[:], in_=vec.rearrange("(g p t) -> p g t", p=P, t=4))

        def load_words(dst, words, k):
            w = dst.shape[2]
            nc.sync.dma_start(
                out=dst[:].bitcast(I32), in_=words[:, :, w * k : w * (k + 1)].bitcast(I32).rearrange("g p w -> p g w")
            )

        nc.scalar.dma_start(out=slope_bf[:], in_=slope.rearrange("(g p t) -> p g t", g=4, t=4))
        make_identity(nc, ident[:])
        nc.vector.memset(g_scales[:].bitcast(I32), 0)
        nc.vector.memset(bs_raw[:].bitcast(I32), 0)
        nc.scalar.activation(out=slope_f[:], in_=slope_bf[:], func=ACT.Identity)
        load_x(0, 0, 1024)
        load_x(0, 1024, 2048)
        load_words(g_words[0], gain_words, 0)
        load_scales(g_scales, gain_scales)
        load_x(1, 0, 2048)
        load_words(g_words[1], gain_words, 1)
        load_x(2, 0, 2048)
        load_vec(lo, u_min)
        load_vec(hi, u_max)
        load_x(3, 0, 2048)
        load_vec(offset_bf, offset)
        load_words(b_raw[0], inmat_words, 0)
        load_x(4, 0, 2048)
        load_words(b_raw[1], inmat_words, 1)
        load_scales(bs_raw, inmat_scales)
        load_x(5, 0, 2048)
        load_x(6, 0, 2048)
        load_x(7, 0, 2048)

        def turn_x(i, a):
            bank = new_bank(("x", i, a))
            words = x_rows[i][:].bitcast(F32)
            for s in range(4):
                g, u = 2 * a + s // 2, s % 2
                nc.tensor.transpose(bank[:, P * s : P * (s + 1)], words[:, 256 * g + u : 256 * (g + 1) : 2], ident[:])

        def x_t_cols(i, a):
            return x_t[i // 4][:, i % 4, 2 * a : 2 * a + 2].rearrange("p g m t -> p (g m t)")

        def copy_x(i, a):
            nc.scalar.copy(
                out=x_t_cols(i, a).bitcast(F32).rearrange("p (g m u) -> p g m u", g=2, u=2),
                in_=live[("x", i, a)][:].rearrange("p (g u m) -> p g m u", g=2, u=2),
            )

        def quant_x(i, a):
            if a == 0:
                live[("xq", i)] = ring.tile([P, 512], U32, name="x_codes", align_bytes=64)
                live[("xs", i)] = ring.tile([P, 512], U8, name="x_scales", align_bytes=64)
            cols = slice(256 * a, 256 * (a + 1))
            nc.vector.quantize_mx(
                out=live[("xq", i)][:, cols].bitcast(FP8X4), scales=live[("xs", i)][:, cols], in_=x_t_cols(i, a)
            )

        def stage1(i, c):
            bank = new_bank(("v", i, c))
            for g in range(4):
                cols = slice(P * g, P * (g + 1))
                nc.tensor.matmul_mx(
                    out=bank[:],
                    lhsT=live[("xq", i)][:, cols].bitcast(FP8X4),
                    lhsT_scale=live[("xs", i)][:, cols],
                    rhs=g_words[c][:, g, :].bitcast(FP4X4),
                    rhs_scale=g_scales[:, g, 512 * c : 512 * (c + 1)],
                    start=(g == 0),
                    stop=(g == 3),
                )

        def copy_v(i, c):
            if c == 0:
                live[("vb", i)] = ring.tile([P, 2, 512], BF16, name="v_rows", align_bytes=64)
            nc.scalar.copy(
                out=live[("vb", i)][:, c, :].rearrange("m (u q e) -> m u q e", u=2, e=2),
                in_=live[("v", i, c)][:].rearrange("m (q u e) -> m u q e", u=2, e=2),
            )

        def turn_v(i):
            bank = new_bank(("vt", i))
            words = live[("vb", i)][:].rearrange("m c k -> m (c k)").bitcast(F32)
            for s in range(4):
                cols = slice(P * s, P * (s + 1))
                nc.tensor.transpose(bank[:, cols], words[:, cols], ident[:])

        def clamp_low(i):
            live[("u", i)] = ring.tile([P, 2, 512], BF16, name="u_t", align_bytes=64)
            pairs = live[("vt", i)][:].bitcast(BF16)
            for c in range(2):
                nc.vector.tensor_tensor(
                    out=live[("u", i)][:, c, :].rearrange("p (m u e) -> p m u e", u=2, e=2),
                    in0=pairs[:, 512 * c : 512 * (c + 1)].rearrange("p (u m e) -> p m u e", u=2, e=2),
                    in1=lo[:, c, :].rearrange("p (o u e) -> p o u e", o=1, u=2).to_broadcast([P, P, 2, 2]),
                    op=ALU.max,
                )

        def clamp_high(i):
            u_t = live[("u", i)][:].rearrange("p c (m t) -> p c m t", t=4)
            nc.vector.tensor_tensor(
                out=u_t,
                in0=u_t,
                in1=hi[:].rearrange("p c (o t) -> p c o t", o=1).to_broadcast([P, 2, P, 4]),
                op=ALU.min,
            )

        def quant_u(i):
            cols = slice(P * (i % 4), P * (i % 4 + 1))
            for c in range(2):
                nc.vector.quantize_mx(
                    out=u_codes[i // 4][:, c, cols].bitcast(FP8X4),
                    scales=u_scales[i // 4][:, c, cols],
                    in_=live[("u", i)][:, c, :],
                )

        def move_words(g):
            src = b_raw[g // 2][:, :, 1024 * (g % 2) : 1024 * (g % 2 + 1)]
            nc.vector.tensor_copy(
                out=b_words[:, g].rearrange("p c (t q b) -> p c t q b", t=4, b=2),
                in_=src.rearrange("p c (q t b) -> p c t q b", t=4, b=2),
            )

        def move_scales(g):
            nc.vector.tensor_copy(
                out=b_scales[:, g].rearrange("p c (t q) -> p c t q", t=4),
                in_=bs_raw[:, :, 512 * g : 512 * (g + 1)].rearrange("p c (q t) -> p c t q", t=4),
            )

        def drift(unit, t, eng):
            h, g = divmod(unit, 4)
            if t == 0:
                live[("y", unit)] = ypool.tile([P, 4, 512], F32, name="y_t", align_bytes=64)
            dst = live[("y", unit)][:, t, :].rearrange("p (j m) -> p j m", j=4)
            src = x_t[h][:, :, g, :, t]
            if eng == 1:
                nc.vector.tensor_scalar(
                    out=dst, in0=src, scalar1=slope_bf[:, g, t : t + 1], scalar2=offset_bf[:, g, t : t + 1],
                    op0=ALU.mult, op1=ALU.add,
                )
            else:
                nc.scalar.activation(
                    out=dst, in_=src, func=ACT.Identity, scale=slope_f[:, g, t : t + 1], bias=offset_bf[:, g, t : t + 1]
                )

        def stage2(unit, t):
            h, g = divmod(unit, 4)
            bank = new_bank(("f", unit, t))
            for c in range(2):
                nc.tensor.matmul_mx(
                    out=bank[:],
                    lhsT=b_words[:, g, c, 256 * t : 256 * (t + 1)].bitcast(FP4X4),
                    lhsT_scale=b_scales[:, g, c, P * t : P * (t + 1)],
                    rhs=u_codes[h][:, c, :].bitcast(FP8X4),
                    rhs_scale=u_scales[h][:, c, :],
                    start=(c == 0),
                    stop=(c == 1),
                )

        def stage2_rows(unit, j):
            h, g = divmod(unit, 4)
            bank = new_bank(("fz", unit, j))
            rows = slice(P * j, P * (j + 1))
            for t in range(4):
                for c in range(2):
                    nc.tensor.matmul_mx(
                        out=bank[:, P * t : P * (t + 1)],
                        lhsT=b_words[:, g, c, 256 * t : 256 * (t + 1)].bitcast(FP4X4),
                        lhsT_scale=b_scales[:, g, c, P * t : P * (t + 1)],
                        rhs=u_codes[h][:, c, rows].bitcast(FP8X4),
                        rhs_scale=u_scales[h][:, c, rows],
                        start=(c == 0),
                        stop=(c == 1),
                    )

        def add_rows(unit, j):
            y_t = live[("y", unit)][:, :, P * j : P * (j + 1)]
            nc.vector.tensor_tensor(
                out=y_t, in0=live[("fz", unit, j)][:].rearrange("p (t m) -> p t m", t=4), in1=y_t, op=ALU.add
            )

        def weave_rows(unit, j):
            if j == 0:
                live[("yb", unit)] = ring.tile([P, 512, 4], BF16, name="y_bf", align_bytes=64)
            rows = slice(P * j, P * (j + 1))
            nc.vector.tensor_copy(
                out=live[("yb", unit)][:, rows, :], in_=live[("y", unit)][:, :, rows].rearrange("p t m -> p m t")
            )

        def quant_rows(unit, j):
            h, g = divmod(unit, 4)
            if j == 0:
                live[("yq", unit)] = ring.tile([P, 512], U32, name="y_codes", align_bytes=64)
            rows = slice(P * j, P * (j + 1))
            nc.vector.quantize_mx(
                out=live[("yq", unit)][:, rows].bitcast(FP8X4),
                scales=y_scales[h][:, g, rows],
                in_=live[("yb", unit)][:, rows, :].rearrange("p m t -> p (m t)"),
            )

        def add(unit, t):
            y_t = live[("y", unit)][:, t, :]
            nc.vector.tensor_tensor(out=y_t, in0=live[("f", unit, t)][:], in1=y_t, op=ALU.add)

        def turn_y(unit, j):
            bank = new_bank(("yr", unit, j))
            for t in range(4):
                nc.tensor.transpose(
                    bank[:, P * t : P * (t + 1)], live[("y", unit)][:, t, P * j : P * (j + 1)], ident[:]
                )

        def copy_y(unit, j, eng):
            h, g = divmod(unit, 4)
            if ("yo", unit) not in live:
                live[("yo", unit)] = ring.tile([P, 4, 512], F32, name="y_rows", align_bytes=64)
            dst = live[("yo", unit)][:, j, :].rearrange("m (p t) -> m p t", t=4)
            src = live[("yr", unit, j)][:].rearrange("m (t p) -> m p t", t=4)
            if eng == 0:
                nc.scalar.copy(out=dst, in_=src)
            else:
                nc.vector.tensor_copy(out=dst, in_=src)

        def store_y(unit, j0, j1):
            h, g = divmod(unit, 4)
            nc.sync.dma_start(
                out=out_0[512 * h + P * j0 : 512 * h + P * j1, 512 * g : 512 * (g + 1)].rearrange("(j m) n -> m j n", m=P),
                in_=live[("yo", unit)][:, j0:j1, :],
            )

        def weave(unit, part):
            if ("yb", unit) not in live:
                live[("yb", unit)] = ring.tile([P, 512, 4], BF16, name="y_bf", align_bytes=64)
            cut = SPLIT[unit]
            cols = slice(0, cut) if part == 0 else slice(cut, 512)
            dst = live[("yb", unit)][:, cols, :]
            src = live[("y", unit)][:, :, cols].rearrange("p t m -> p m t")
            if part == 0:
                nc.vector.tensor_copy(out=dst, in_=src)
            else:
                nc.scalar.copy(out=dst, in_=src)

        def quant_y(unit):
            h, g = divmod(unit, 4)
            live[("yq", unit)] = ring.tile([P, 512], U32, name="y_codes", align_bytes=64)
            nc.vector.quantize_mx(
                out=live[("yq", unit)][:].bitcast(FP8X4),
                scales=y_scales[h][:, g, :],
                in_=live[("yb", unit)][:].rearrange("p m t -> p (m t)"),
            )

        def store_codes(unit, m0, m1):
            h, g = divmod(unit, 4)
            nc.sync.dma_start(
                out=out_1[g, :, 512 * h + P * m0 : 512 * h + P * m1, :].rearrange("p m t -> p (m t)").bitcast(I32),
                in_=live[("yq", unit)][:, P * m0 : P * m1].bitcast(I32),
            )

        def store_scales(h, g0, g1):
            for q in range(4):
                nc.sync.dma_start(
                    out=out_2[g0:g1, 4 * q : 4 * q + 4, 512 * h : 512 * (h + 1)].bitcast(I32).rearrange("g r w -> r g w"),
                    in_=y_scales[h][32 * q : 32 * q + 4, g0:g1, :].bitcast(I32),
                )

        steps = {
            "XT": turn_x, "CX": copy_x, "QX": quant_x, "S1": stage1, "CU": copy_v, "UT": turn_v, "MX": clamp_low,
            "MN": clamp_high, "QU": quant_u, "PW": move_words, "PS": move_scales, "DR": drift, "S2": stage2,
            "AD": add, "YT": turn_y, "CY": copy_y, "SY": store_y, "IL": weave, "QY": quant_y, "SC": store_codes,
            "SS": store_scales, "Z2": stage2_rows, "ZA": add_rows, "ZI": weave_rows, "ZQ": quant_rows, "ZT": turn_y,
        }
        for word in ORDER:
            name, args = word.split(":")
            steps[name](*[int(a) for a in args.split(",")])
